import numpy as np
import ml_dtypes


def mxq(x, axis, fmt="e4m3"):
    dtype, down = {"e4m3": (ml_dtypes.float8_e4m3fn, 7), "e5m2": (ml_dtypes.float8_e5m2, 14)}[fmt]
    v = np.moveaxis(np.asarray(x, np.float32).astype(ml_dtypes.bfloat16).astype(np.float64), axis, -1)
    blocks = v.reshape(v.shape[:-1] + (-1, 32))
    amax = np.abs(blocks).max(-1, keepdims=True)
    byte = np.maximum(np.where(amax > 0, np.frexp(amax)[1] - 1 + 127, 0) - down, 1)
    scale = np.exp2(byte - 127.0)
    codes = (blocks / scale).astype(np.float32).astype(dtype).astype(np.float64)
    return np.moveaxis((codes * scale).reshape(v.shape), -1, axis)


WIDE = False


def mx_kscale(k):
    if not WIDE:
        return np.ones(k)
    levels = np.array([10, -10, 5, -5, 0])
    if k % 512:
        return np.exp2(np.random.permutation(np.resize(levels, k // 32))).repeat(32)
    a = np.empty((k // 512, 16))
    for p in range(k // 512):
        a[p, :8] = np.random.permutation(np.resize(levels, 8))
        for g in range(8):
            far = levels[np.abs(levels - a[p, g]) >= 10]
            a[p, g + 8] = far[np.random.randint(len(far))]
    return np.exp2(a.ravel()).repeat(32)


def f64(x):
    return np.asarray(x).astype(np.float64)


def striped(idx):
    return np.tile(idx.reshape(-1, 16).T, (8, 1)).astype(np.uint16)


def unstriped(offs):
    return offs[:16].T.reshape(-1).astype(np.int64)


E2M1 = np.array([0.0, 0.5, 1.0, 1.5, 2.0, 3.0, 4.0, 6.0, -0.0, -0.5, -1.0, -1.5, -2.0, -3.0, -4.0, -6.0])


def pack_weight(w, fmt):
    k, n = w.shape
    w = f64(np.asarray(w, np.float32).astype(ml_dtypes.bfloat16)).reshape(k // 32, 32, n)
    amax = np.abs(w).max(1)
    if fmt == "e4m3":
        byte = np.frexp(amax)[1] - 1 + 127 - 7
    else:
        mant, ex = np.frexp(amax / 6.0)
        byte = np.where(mant > 0.5, ex, ex - 1) + 127
    byte = np.clip(np.where(amax > 0, byte, 1), 1, 254)
    scaled = (w * np.exp2(127.0 - byte)[:, None, :]).reshape(k, n).astype(np.float32)
    by_word = np.ascontiguousarray(scaled.reshape(k // 512, 128, 4, n).transpose(0, 1, 3, 2))
    if fmt == "e4m3":
        words = by_word.astype(ml_dtypes.float8_e4m3fn).view(np.uint8)
    else:
        c = by_word.astype(ml_dtypes.float4_e2m1fn).view(np.uint8) & 0xF
        words = (c[..., 0::2] | (c[..., 1::2] << 4)).reshape(k // 512, 128, 2 * n)
    return np.ascontiguousarray(words), np.ascontiguousarray(byte.astype(np.uint8).reshape(k // 512, 16, n))


def unpack_weight(words, scales, fmt):
    g, _, n = scales.shape
    words = np.ascontiguousarray(words).reshape(g, 128, n, -1)
    if fmt == "e4m3":
        vals = words.view(ml_dtypes.float8_e4m3fn).astype(np.float64)
    else:
        nib = np.empty((g, 128, n, 4), np.uint8)
        nib[..., 0::2] = words & 0xF
        nib[..., 1::2] = words >> 4
        vals = E2M1[nib]
    vals = vals * np.repeat(np.exp2(scales.astype(np.float64) - 127.0), 8, axis=1)[..., None]
    return vals.transpose(0, 1, 3, 2).reshape(g * 512, n)


def gelu(v):
    return 0.5 * v * (1.0 + np.tanh(np.sqrt(2.0 / np.pi) * (v + 0.044715 * v**3)))


K, T, S, H, N, T2, R = 512, 2048, 1024, 1536, 512, 2048, 128

def setup_inputs():
    n = np.random.standard_normal
    s = mx_kscale(K)[:, None]
    u = mx_kscale(H)[:, None]
    tab_words, tab_scales = pack_weight(n((K, T)) * s, "e4m3")
    wa_words, wa_scales = pack_weight(n((K, H)) / s * u.T * 0.7 / np.sqrt(K), "e2m1")
    wb = n((K, H)) / s * u.T * 0.7 / np.sqrt(K)
    wc = n((H, N)) / u * 1.2 / np.sqrt(H)
    return {
        "tab_words": tab_words, "tab_scales": tab_scales,
        "offs": striped(np.random.permutation(T)[:S]),
        "offs2": striped(np.random.permutation(T)[:S]),
        "offs3": striped(np.random.permutation(T2)[:S]),
        "wa_words": wa_words, "wa_scales": wa_scales,
        "wb": wb.astype(np.float32),
        "wc": wc.astype(np.float32),
        "bias": (0.6 * n(N)).astype(np.float32),
        "wgo": np.exp(0.3 * n((R, S))).astype(np.float32),
    }

def reference(tab_words, tab_scales, offs, offs2, offs3, wa_words, wa_scales, wb, wc, bias, wgo):
    TW = unpack_weight(tab_words, tab_scales, "e4m3")
    v = TW[:, unstriped(offs)]
    v2 = TW[:, unstriped(offs2)]
    wa = unpack_weight(wa_words, wa_scales, "e2m1")
    d = wa.T @ v - mxq(f64(wb), 0, "e4m3").T @ v2
    h = np.abs(d)
    e = mxq(f64(wc), 0, "e4m3").T @ mxq(h, 0, "e4m3")
    y = np.tanh(e + f64(bias)[:, None])
    out = np.zeros((N, T2))
    out[:, unstriped(offs3)] = np.tile(f64(wgo), (N // R, 1)) * y
    return out

@@ -1,0 +1,265 @@
+from contextlib import ExitStack
+
+import concourse.mybir as mybir
+
+K, T, S, H, N, T2 = 512, 2048, 1024, 1536, 512, 2048
+FLOPS = 2 * (2 * K * H * S + H * N * S)
+
+F32 = mybir.dt.float32
+BF16 = mybir.dt.bfloat16
+I32 = mybir.dt.int32
+U32 = mybir.dt.uint32
+U16 = mybir.dt.uint16
+U8 = mybir.dt.uint8
+E4M3 = mybir.dt.float8_e4m3fn_x4
+E2M1 = mybir.dt.float4_e2m1fn_x4
+ACT = mybir.ActivationFunctionType
+ALU = mybir.AluOpType
+
+P = 128
+PACK = 4
+PASS = P * PACK
+R_PASSES = H // PASS
+N_TILES = N // P
+CHUNK = 256
+CHUNKS = S // CHUNK
+SUB = 128
+GAP_BANKS = 6
+FEATURE_BANKS = 2
+
+
+def tile_list_peering_request_board_kernel(
+    tc, tab_words, tab_scales, offs, offs2, offs3, wa_words, wa_scales, wb, wc, bias, wgo, out
+):
+    nc = tc.nc
+    with ExitStack() as ctx:
+        keep = ctx.enter_context(tc.tile_pool(name="keep", bufs=1))
+        ring = ctx.enter_context(tc.tile_pool(name="ring", bufs=2))
+        psum = ctx.enter_context(tc.psum_pool(name="psum", bufs=1))
+
+        req_list = keep.tile([P, S // 16], U16, name="req_list")
+        peer_list = keep.tile([P, S // 16], U16, name="peer_list")
+        board_list = keep.tile([P, S // 16], U16, name="board_list")
+        tab_plane = keep.tile([P, T], U8, name="tab_plane", align_bytes=64)
+        wa_plane_raw = keep.tile([P, H], U8, name="wa_plane_raw", align_bytes=64)
+        tab_codes = keep.tile([P, T], I32, name="tab_codes", align_bytes=64)
+        wa_raw = keep.tile([P, 2 * H], U8, name="wa_raw", align_bytes=64)
+        req_plane = keep.tile([P, S], U8, name="req_plane", align_bytes=64)
+        peer_plane = keep.tile([P, S], U8, name="peer_plane", align_bytes=64)
+        bias_cols = keep.tile([P, N_TILES], F32, name="bias_cols")
+        pages = [keep.tile([P, T2], F32, name=f"page{n}") for n in range(N_TILES)]
+        gap_banks = [psum.tile([P, PACK, SUB], F32, name=f"gap_bank{i}") for i in range(GAP_BANKS)]
+        feature_banks = [psum.tile([P, 2 * CHUNK], F32, name=f"feature_bank{i}") for i in range(FEATURE_BANKS)]
+
+        def load_scale_rows(queue, plane, rows):
+            for q in range(4):
+                queue.dma_start(out=plane[32 * q : 32 * q + 4, :].bitcast(I32), in_=rows[0, 4 * q : 4 * q + 4, :].bitcast(I32))
+
+        nc.gpsimd.memset(tab_plane[:].bitcast(I32), 0)
+        nc.gpsimd.memset(wa_plane_raw[:].bitcast(I32), 0)
+        load_scale_rows(nc.scalar, tab_plane, tab_scales)
+        nc.sync.dma_start(req_list[:], offs)
+        nc.sync.dma_start(peer_list[:], offs2)
+
+        wb_rows = wb.rearrange("(p j) r -> p j r", j=PACK)
+        half = PASS // 2
+        wb_raw = {}
+
+        def load_wb(b):
+            for u in range(2):
+                wb_raw[b, u] = keep.tile([P, PACK, half], F32, name=f"wb_raw{b}{u}")
+                c0 = b * PASS + u * half
+                nc.sync.dma_start(out=wb_raw[b, u][:], in_=wb_rows[:, :, c0 : c0 + half])
+
+        wc_raw = {}
+
+        def load_wc(n0, count):
+            for b in range(R_PASSES):
+                raw = keep.tile([P, PACK, count * P], F32, name=f"wc_raw{n0}{b}")
+                rows = wc[b * PASS : (b + 1) * PASS, n0 * P : (n0 + count) * P]
+                nc.sync.dma_start(out=raw[:], in_=rows.rearrange("(p j) n -> p j n", j=PACK))
+                for i in range(count):
+                    wc_raw[n0 + i, b] = raw[:, :, i * P : (i + 1) * P]
+
+        wgo_parts = []
+
+        def load_wgo(c0, count):
+            part = keep.tile([P, count * CHUNK], F32, name=f"wgo{c0}")
+            nc.sync.dma_start(out=part[:], in_=wgo[:, c0 * CHUNK : (c0 + count) * CHUNK])
+            for i in range(count):
+                wgo_parts.append(part[:, i * CHUNK : (i + 1) * CHUNK])
+
+        load_wb(0)
+        nc.sync.dma_start(out=wa_raw[:].bitcast(I32), in_=wa_words[0].bitcast(I32))
+        load_scale_rows(nc.sync, wa_plane_raw, wa_scales)
+        nc.sync.dma_start(out=tab_codes[:], in_=tab_words[0].rearrange("p t i -> p (t i)").bitcast(I32))
+        load_wb(1)
+        load_wb(2)
+        load_wc(0, 1)
+        nc.sync.dma_start(board_list[:], offs3)
+        with nc.allow_non_contiguous_dma(reason="one bias value a partition"):
+            nc.sync.dma_start(out=bias_cols[:], in_=bias.rearrange("(n p) -> p n", p=P))
+        load_wgo(0, 1)
+        load_wc(1, 1)
+        load_wgo(1, 3)
+        load_wc(2, 2)
+
+        for page in pages:
+            for c0 in range(0, T2, 512):
+                nc.gpsimd.memset(page[:, c0 : c0 + 512], 0.0)
+
+        nc.vector.tensor_copy(req_plane[:], tab_plane[:].indirect(req_list[:]))
+        nc.vector.tensor_copy(peer_plane[:], tab_plane[:].indirect(peer_list[:]))
+
+        wa_codes, wa_plane = {}, {}
+
+        def deal_wa(b):
+            wa_codes[b] = keep.tile([P, 2 * PASS], U8, name=f"wa_codes{b}", align_bytes=64)
+            wa_plane[b] = keep.tile([P, PASS], U8, name=f"wa_plane{b}", align_bytes=64)
+            cols = slice(b * PASS, (b + 1) * PASS)
+            nc.vector.tensor_copy(
+                out=wa_codes[b][:].bitcast(U16).rearrange("p (t m) -> p m t", t=PACK),
+                in_=wa_raw[:].bitcast(U16)[:, cols].rearrange("p (m t) -> p m t", t=PACK),
+            )
+            nc.vector.tensor_copy(
+                out=wa_plane[b][:].rearrange("p (t m) -> p m t", t=PACK),
+                in_=wa_plane_raw[:, cols].rearrange("p (m t) -> p m t", t=PACK),
+            )
+
+        wb_codes, wb_plane = {}, {}
+
+        def quantise_wb(b):
+            grouped = keep.tile([P, PACK, P, PACK], BF16, name=f"wb_grouped{b}", align_bytes=64)
+            for u in range(2):
+                dst = grouped[:, :, u * (P // 2) : (u + 1) * (P // 2), :].rearrange("p t m j -> p m t j")
+                src = wb_raw[b, u][:].rearrange("p j (m t) -> p m t j", t=PACK)
+                if (b, u) == (R_PASSES - 1, 1):
+                    nc.vector.tensor_scalar(out=dst, in0=src, scalar1=-1.0, scalar2=None, op0=ALU.mult)
+                else:
+                    nc.scalar.activation(out=dst, in_=src, func=ACT.Copy, scale=-1.0)
+            wb_codes[b] = keep.tile([P, PASS], U32, name=f"wb_codes{b}", align_bytes=64)
+            wb_plane[b] = keep.tile([P, PASS], U8, name=f"wb_plane{b}", align_bytes=64)
+            nc.vector.quantize_mx(
+                out=wb_codes[b][:].bitcast(E4M3), scales=wb_plane[b][:], in_=grouped[:].rearrange("p t m j -> p (t m j)")
+            )
+
+        wc_codes, wc_plane = {}, {}
+
+        def quantise_wc(n):
+            grouped = ring.tile([P, R_PASSES, P, PACK], BF16, name="wc_grouped", align_bytes=64)
+            for b in range(R_PASSES):
+                nc.scalar.activation(
+                    out=grouped[:, b, :, :].rearrange("p (c i) j -> p c j i", i=4),
+                    in_=wc_raw[n, b].rearrange("p j (c i) -> p c j i", i=4),
+                    func=ACT.Copy,
+                )
+            wc_codes[n] = keep.tile([P, R_PASSES * P], U32, name=f"wc_codes{n}", align_bytes=64)
+            wc_plane[n] = keep.tile([P, R_PASSES * P], U8, name=f"wc_plane{n}", align_bytes=64)
+            nc.vector.quantize_mx(
+                out=wc_codes[n][:].bitcast(E4M3), scales=wc_plane[n][:], in_=grouped[:].rearrange("p b n j -> p (b n j)")
+            )
+
+        gathered = {}
+
+        def gather_words(c):
+            cols = slice(c * CHUNK // 16, (c + 1) * CHUNK // 16)
+            req = ring.tile([P, CHUNK], U32, name="req_codes", align_bytes=64)
+            peer = ring.tile([P, CHUNK], U32, name="peer_codes", align_bytes=64)
+            nc.vector.tensor_copy(req[:], tab_codes[:].bitcast(U32).indirect(req_list[:, cols]))
+            nc.vector.tensor_copy(peer[:], tab_codes[:].bitcast(U32).indirect(peer_list[:, cols]))
+            gathered[c] = (req, peer)
+
+        h_codes, h_plane = {}, {}
+        turn = {"gap": 0, "feature": 0}
+
+        def gap_pass(c, b):
+            req, peer = gathered[c]
+            grouped = keep.tile([P, CHUNK, PACK], BF16, name=f"h_grouped{c}{b}", align_bytes=64)
+            for s in range(CHUNK // SUB):
+                bank = gap_banks[turn["gap"] % GAP_BANKS]
+                turn["gap"] = turn["gap"] + 1
+                local = slice(s * SUB, (s + 1) * SUB)
+                entries = slice(c * CHUNK + s * SUB, c * CHUNK + (s + 1) * SUB)
+                for t in range(PACK):
+                    col = t * P
+                    nc.tensor.matmul_mx(
+                        out=bank[:, t, :],
+                        lhsT=wa_codes[b][:, 2 * col : 2 * (col + P)].bitcast(E2M1),
+                        lhsT_scale=wa_plane[b][:, col : col + P],
+                        rhs=req[:, local].bitcast(E4M3),
+                        rhs_scale=req_plane[:, entries],
+                        start=(t == 0),
+                        stop=False,
+                    )
+                for t in range(PACK):
+                    nc.tensor.matmul_mx(
+                        out=bank[:, t, :],
+                        lhsT=wb_codes[b][:, t * P : (t + 1) * P].bitcast(E4M3),
+                        lhsT_scale=wb_plane[b][:, t * P : (t + 1) * P],
+                        rhs=peer[:, local].bitcast(E4M3),
+                        rhs_scale=peer_plane[:, entries],
+                        start=False,
+                        stop=(t == PACK - 1),
+                    )
+                nc.scalar.activation(out=grouped[:, local, :], in_=bank[:].rearrange("p t j -> p j t"), func=ACT.Abs)
+            h_codes[c, b] = keep.tile([P, CHUNK], U32, name=f"h_codes{c}{b}", align_bytes=64)
+            h_plane[c, b] = keep.tile([P, CHUNK], U8, name=f"h_plane{c}{b}", align_bytes=64)
+            nc.vector.quantize_mx(
+                out=h_codes[c, b][:].bitcast(E4M3), scales=h_plane[c, b][:], in_=grouped[:].rearrange("p j t -> p (j t)")
+            )
+
+        def gap_chunk(c):
+            for b in range(R_PASSES):
+                gap_pass(c, b)
+
+        def place(n, c):
+            bank = feature_banks[turn["feature"] % FEATURE_BANKS]
+            turn["feature"] = turn["feature"] + 1
+            for b in range(R_PASSES):
+                nc.tensor.matmul_mx(
+                    out=bank[:, 0:CHUNK],
+                    lhsT=wc_codes[n][:, b * P : (b + 1) * P].bitcast(E4M3),
+                    lhsT_scale=wc_plane[n][:, b * P : (b + 1) * P],
+                    rhs=h_codes[c, b][:].bitcast(E4M3),
+                    rhs_scale=h_plane[c, b][:],
+                    start=(b == 0),
+                    stop=(b == R_PASSES - 1),
+                )
+            y = keep.tile([P, CHUNK], F32, name=f"y{n}{c}")
+            nc.scalar.activation(out=y[:], in_=bank[:, 0:CHUNK], func=ACT.Tanh, bias=bias_cols[:, n : n + 1])
+            cols = slice(c * CHUNK // 16, (c + 1) * CHUNK // 16)
+            nc.vector.tensor_tensor(pages[n][:].indirect(board_list[:, cols]), y[:], wgo_parts[c], ALU.mult)
+            if c == CHUNKS - 1:
+                nc.sync.dma_start(out=out[n * P : (n + 1) * P, :], in_=pages[n][:])
+
+        for b in range(R_PASSES):
+            deal_wa(b)
+        gather_words(0)
+        gather_words(1)
+        for b in range(R_PASSES):
+            quantise_wb(b)
+            gap_pass(0, b)
+        quantise_wc(0)
+        place(0, 0)
+        gather_words(2)
+        quantise_wc(1)
+        place(1, 0)
+        gap_chunk(1)
+        gather_words(3)
+        place(0, 1)
+        place(1, 1)
+        quantise_wc(2)
+        place(2, 0)
+        place(2, 1)
+        quantise_wc(3)
+        place(3, 0)
+        gap_chunk(2)
+        place(3, 1)
+        place(0, 2)
+        gap_chunk(3)
+        place(1, 2)
+        place(0, 3)
+        place(1, 3)
+        for n in (2, 3):
+            place(n, 2)
+            place(n, 3)

@@ -44,10 +44,8 @@ def tile_list_peering_request_board_kernel(
         wa_plane_raw = keep.tile([P, H], U8, name="wa_plane_raw", align_bytes=64)
         tab_codes = keep.tile([P, T], I32, name="tab_codes", align_bytes=64)
         wa_raw = keep.tile([P, 2 * H], U8, name="wa_raw", align_bytes=64)
-        req_plane = keep.tile([P, S], U8, name="req_plane", align_bytes=64)
-        peer_plane = keep.tile([P, S], U8, name="peer_plane", align_bytes=64)
         bias_cols = keep.tile([P, N_TILES], F32, name="bias_cols")
-        pages = [keep.tile([P, T2], F32, name=f"page{n}") for n in range(N_TILES)]
+        pages = [keep.tile([P, T2], F32, name=f"page{n}") for n in range(N_TILES - 1)]
         gap_banks = [psum.tile([P, PACK, SUB], F32, name=f"gap_bank{i}") for i in range(GAP_BANKS)]
         feature_banks = [psum.tile([P, 2 * CHUNK], F32, name=f"feature_bank{i}") for i in range(FEATURE_BANKS)]
 
@@ -67,9 +65,21 @@ def tile_list_peering_request_board_kernel(
 
         def load_wb(b):
             for u in range(2):
-                wb_raw[b, u] = keep.tile([P, PACK, half], F32, name=f"wb_raw{b}{u}")
+                wb_raw[b, u] = keep.tile([P, PACK, half], F32, name=f"wb_raw{b}{u}", tag=f"wb_raw{b}{u}", align_bytes=64)
                 c0 = b * PASS + u * half
                 nc.sync.dma_start(out=wb_raw[b, u][:], in_=wb_rows[:, :, c0 : c0 + half])
+
+        def load_small():
+            nc.sync.dma_start(board_list[:], offs3)
+            with nc.allow_non_contiguous_dma(reason="one bias value a partition"):
+                nc.sync.dma_start(out=bias_cols[:], in_=bias.rearrange("(n p) -> p n", p=P))
+
+        def load_wa():
+            nc.sync.dma_start(out=wa_raw[:].bitcast(I32), in_=wa_words[0].bitcast(I32))
+            load_scale_rows(nc.sync, wa_plane_raw, wa_scales)
+
+        def load_tab():
+            nc.sync.dma_start(out=tab_codes[:], in_=tab_words[0].rearrange("p t i -> p (t i)").bitcast(I32))
 
         wc_raw = {}
 
@@ -81,35 +91,21 @@ def tile_list_peering_request_board_kernel(
                 for i in range(count):
                     wc_raw[n0 + i, b] = raw[:, :, i * P : (i + 1) * P]
 
-        wgo_parts = []
-
-        def load_wgo(c0, count):
-            part = keep.tile([P, count * CHUNK], F32, name=f"wgo{c0}")
-            nc.sync.dma_start(out=part[:], in_=wgo[:, c0 * CHUNK : (c0 + count) * CHUNK])
-            for i in range(count):
-                wgo_parts.append(part[:, i * CHUNK : (i + 1) * CHUNK])
-
+        wgo_sb = keep.tile([P, S], F32, name="wgo_sb")
         load_wb(0)
-        nc.sync.dma_start(out=wa_raw[:].bitcast(I32), in_=wa_words[0].bitcast(I32))
-        load_scale_rows(nc.sync, wa_plane_raw, wa_scales)
-        nc.sync.dma_start(out=tab_codes[:], in_=tab_words[0].rearrange("p t i -> p (t i)").bitcast(I32))
         load_wb(1)
+        load_wa()
+        load_tab()
         load_wb(2)
         load_wc(0, 1)
-        nc.sync.dma_start(board_list[:], offs3)
-        with nc.allow_non_contiguous_dma(reason="one bias value a partition"):
-            nc.sync.dma_start(out=bias_cols[:], in_=bias.rearrange("(n p) -> p n", p=P))
-        load_wgo(0, 1)
+        load_small()
+        nc.sync.dma_start(out=wgo_sb[:, 0:CHUNK], in_=wgo[:, 0:CHUNK])
         load_wc(1, 1)
-        load_wgo(1, 3)
+        nc.sync.dma_start(out=wgo_sb[:, CHUNK:S], in_=wgo[:, CHUNK:S])
         load_wc(2, 2)
 
         for page in pages:
-            for c0 in range(0, T2, 512):
-                nc.gpsimd.memset(page[:, c0 : c0 + 512], 0.0)
-
-        nc.vector.tensor_copy(req_plane[:], tab_plane[:].indirect(req_list[:]))
-        nc.vector.tensor_copy(peer_plane[:], tab_plane[:].indirect(peer_list[:]))
+            nc.vector.memset(page[:], 0.0)
 
         wa_codes, wa_plane = {}, {}
 
@@ -129,14 +125,11 @@ def tile_list_peering_request_board_kernel(
         wb_codes, wb_plane = {}, {}
 
         def quantise_wb(b):
-            grouped = keep.tile([P, PACK, P, PACK], BF16, name=f"wb_grouped{b}", align_bytes=64)
+            grouped = keep.tile([P, PACK, P, PACK], BF16, name=f"wb_grouped{b}", tag=f"wb_grouped{b}", align_bytes=64)
             for u in range(2):
                 dst = grouped[:, :, u * (P // 2) : (u + 1) * (P // 2), :].rearrange("p t m j -> p m t j")
                 src = wb_raw[b, u][:].rearrange("p j (m t) -> p m t j", t=PACK)
-                if (b, u) == (R_PASSES - 1, 1):
-                    nc.vector.tensor_scalar(out=dst, in0=src, scalar1=-1.0, scalar2=None, op0=ALU.mult)
-                else:
-                    nc.scalar.activation(out=dst, in_=src, func=ACT.Copy, scale=-1.0)
+                nc.scalar.activation(out=dst, in_=src, func=ACT.Copy, scale=-1.0)
             wb_codes[b] = keep.tile([P, PASS], U32, name=f"wb_codes{b}", align_bytes=64)
             wb_plane[b] = keep.tile([P, PASS], U8, name=f"wb_plane{b}", align_bytes=64)
             nc.vector.quantize_mx(
@@ -159,27 +152,36 @@ def tile_list_peering_request_board_kernel(
                 out=wc_codes[n][:].bitcast(E4M3), scales=wc_plane[n][:], in_=grouped[:].rearrange("p b n j -> p (b n j)")
             )
 
-        gathered = {}
+        looked_up = {}
 
-        def gather_words(c):
-            cols = slice(c * CHUNK // 16, (c + 1) * CHUNK // 16)
-            req = ring.tile([P, CHUNK], U32, name="req_codes", align_bytes=64)
-            peer = ring.tile([P, CHUNK], U32, name="peer_codes", align_bytes=64)
-            nc.vector.tensor_copy(req[:], tab_codes[:].bitcast(U32).indirect(req_list[:, cols]))
-            nc.vector.tensor_copy(peer[:], tab_codes[:].bitcast(U32).indirect(peer_list[:, cols]))
-            gathered[c] = (req, peer)
+        def gather(kind, window, places, dtype, c0, count, slot):
+            picked = keep.tile([P, count * CHUNK], dtype, name=f"{kind}{c0}", tag=slot, align_bytes=64)
+            cols = slice(c0 * CHUNK // 16, (c0 + count) * CHUNK // 16)
+            nc.vector.tensor_copy(picked[:], window.indirect(places[:, cols]))
+            for i in range(count):
+                looked_up[kind, c0 + i] = picked[:, i * CHUNK : (i + 1) * CHUNK]
+
+        def gather_scales(c0, count, slots):
+            gather("req_plane", tab_plane[:], req_list, U8, c0, count, slots[0])
+            gather("peer_plane", tab_plane[:], peer_list, U8, c0, count, slots[1])
+
+        def gather_req(c0, count, slot):
+            gather("req_codes", tab_codes[:].bitcast(U32), req_list, U32, c0, count, slot)
+
+        def gather_peer(c0, count, slot):
+            gather("peer_codes", tab_codes[:].bitcast(U32), peer_list, U32, c0, count, slot)
 
         h_codes, h_plane = {}, {}
         turn = {"gap": 0, "feature": 0}
 
         def gap_pass(c, b):
-            req, peer = gathered[c]
-            grouped = keep.tile([P, CHUNK, PACK], BF16, name=f"h_grouped{c}{b}", align_bytes=64)
+            req, peer = looked_up["req_codes", c], looked_up["peer_codes", c]
+            req_plane, peer_plane = looked_up["req_plane", c], looked_up["peer_plane", c]
+            grouped = keep.tile([P, CHUNK, PACK], BF16, name=f"h_grouped{c}{b}", tag=f"h_grouped{c}{b}", align_bytes=64)
             for s in range(CHUNK // SUB):
                 bank = gap_banks[turn["gap"] % GAP_BANKS]
                 turn["gap"] = turn["gap"] + 1
                 local = slice(s * SUB, (s + 1) * SUB)
-                entries = slice(c * CHUNK + s * SUB, c * CHUNK + (s + 1) * SUB)
                 for t in range(PACK):
                     col = t * P
                     nc.tensor.matmul_mx(
@@ -187,7 +189,7 @@ def tile_list_peering_request_board_kernel(
                         lhsT=wa_codes[b][:, 2 * col : 2 * (col + P)].bitcast(E2M1),
                         lhsT_scale=wa_plane[b][:, col : col + P],
                         rhs=req[:, local].bitcast(E4M3),
-                        rhs_scale=req_plane[:, entries],
+                        rhs_scale=req_plane[:, local],
                         start=(t == 0),
                         stop=False,
                     )
@@ -197,7 +199,7 @@ def tile_list_peering_request_board_kernel(
                         lhsT=wb_codes[b][:, t * P : (t + 1) * P].bitcast(E4M3),
                         lhsT_scale=wb_plane[b][:, t * P : (t + 1) * P],
                         rhs=peer[:, local].bitcast(E4M3),
-                        rhs_scale=peer_plane[:, entries],
+                        rhs_scale=peer_plane[:, local],
                         start=False,
                         stop=(t == PACK - 1),
                     )
@@ -212,54 +214,63 @@ def tile_list_peering_request_board_kernel(
             for b in range(R_PASSES):
                 gap_pass(c, b)
 
-        def place(n, c):
+        def place(n, c0, count):
             bank = feature_banks[turn["feature"] % FEATURE_BANKS]
             turn["feature"] = turn["feature"] + 1
-            for b in range(R_PASSES):
-                nc.tensor.matmul_mx(
-                    out=bank[:, 0:CHUNK],
-                    lhsT=wc_codes[n][:, b * P : (b + 1) * P].bitcast(E4M3),
-                    lhsT_scale=wc_plane[n][:, b * P : (b + 1) * P],
-                    rhs=h_codes[c, b][:].bitcast(E4M3),
-                    rhs_scale=h_plane[c, b][:],
-                    start=(b == 0),
-                    stop=(b == R_PASSES - 1),
-                )
-            y = keep.tile([P, CHUNK], F32, name=f"y{n}{c}")
-            nc.scalar.activation(out=y[:], in_=bank[:, 0:CHUNK], func=ACT.Tanh, bias=bias_cols[:, n : n + 1])
-            cols = slice(c * CHUNK // 16, (c + 1) * CHUNK // 16)
-            nc.vector.tensor_tensor(pages[n][:].indirect(board_list[:, cols]), y[:], wgo_parts[c], ALU.mult)
-            if c == CHUNKS - 1:
-                nc.sync.dma_start(out=out[n * P : (n + 1) * P, :], in_=pages[n][:])
+            for i in range(count):
+                for b in range(R_PASSES):
+                    nc.tensor.matmul_mx(
+                        out=bank[:, i * CHUNK : (i + 1) * CHUNK],
+                        lhsT=wc_codes[n][:, b * P : (b + 1) * P].bitcast(E4M3),
+                        lhsT_scale=wc_plane[n][:, b * P : (b + 1) * P],
+                        rhs=h_codes[c0 + i, b][:].bitcast(E4M3),
+                        rhs_scale=h_plane[c0 + i, b][:],
+                        start=(b == 0),
+                        stop=(b == R_PASSES - 1),
+                    )
+            width = count * CHUNK
+            y = keep.tile([P, width], F32, name=f"y{n}{c0}")
+            nc.scalar.activation(out=y[:], in_=bank[:, 0:width], func=ACT.Tanh, bias=bias_cols[:, n : n + 1])
+            first = c0 * CHUNK
+            places = board_list[:, first // 16 : (first + width) // 16]
+            nc.vector.tensor_tensor(pages[n % len(pages)][:].indirect(places), y[:], wgo_sb[:, first : first + width], ALU.mult)
+            if c0 + count == CHUNKS:
+                nc.sync.dma_start(out=out[n * P : (n + 1) * P, :], in_=pages[n % len(pages)][:])
 
-        for b in range(R_PASSES):
-            deal_wa(b)
-        gather_words(0)
-        gather_words(1)
-        for b in range(R_PASSES):
-            quantise_wb(b)
-            gap_pass(0, b)
+        gather_scales(0, 2, ("rp0", "pp0"))
+        quantise_wb(0)
+        deal_wa(0)
+        quantise_wb(1)
+        deal_wa(1)
+        deal_wa(2)
+        gather_req(0, 1, "rc0")
+        gather_peer(0, 1, "pc0")
+        quantise_wb(2)
+        gather_req(1, 1, "rc1")
+        gather_peer(1, 1, "pc1")
+        gap_pass(0, 0)
+        gap_pass(0, 1)
         quantise_wc(0)
-        place(0, 0)
-        gather_words(2)
+        gap_pass(0, 2)
+        gather_scales(2, 2, ("wb_grouped2", "wb_raw21"))
         quantise_wc(1)
-        place(1, 0)
+        place(0, 0, 1)
+        gather_req(2, 2, "h_grouped02")
+        place(1, 0, 1)
         gap_chunk(1)
-        gather_words(3)
-        place(0, 1)
-        place(1, 1)
+        gather_peer(2, 2, "h_grouped12")
+        place(0, 1, 1)
         quantise_wc(2)
-        place(2, 0)
-        place(2, 1)
-        quantise_wc(3)
-        place(3, 0)
+        place(1, 1, 1)
+        place(2, 0, 1)
         gap_chunk(2)
-        place(3, 1)
-        place(0, 2)
+        place(2, 1, 1)
+        place(0, 2, 1)
         gap_chunk(3)
-        place(1, 2)
-        place(0, 3)
-        place(1, 3)
-        for n in (2, 3):
-            place(n, 2)
-            place(n, 3)
+        place(1, 2, 1)
+        place(0, 3, 1)
+        quantise_wc(3)
+        place(1, 3, 1)
+        place(2, 2, 2)
+        place(3, 0, 2)
+        place(3, 2, 2)

@@ -34,14 +34,13 @@ def tile_list_peering_request_board_kernel(
     nc = tc.nc
     with ExitStack() as ctx:
         keep = ctx.enter_context(tc.tile_pool(name="keep", bufs=1))
-        ring = ctx.enter_context(tc.tile_pool(name="ring", bufs=2))
         psum = ctx.enter_context(tc.psum_pool(name="psum", bufs=1))
 
         req_list = keep.tile([P, S // 16], U16, name="req_list")
         peer_list = keep.tile([P, S // 16], U16, name="peer_list")
         board_list = keep.tile([P, S // 16], U16, name="board_list")
         tab_plane = keep.tile([P, T], U8, name="tab_plane", align_bytes=64)
-        wa_plane_raw = keep.tile([P, H], U8, name="wa_plane_raw", align_bytes=64)
+        wa_plane_raw = keep.tile([P, H], U8, name="wa_plane_raw", tag="wa_plane_raw", align_bytes=64)
         tab_codes = keep.tile([P, T], I32, name="tab_codes", align_bytes=64)
         wa_raw = keep.tile([P, 2 * H], U8, name="wa_raw", align_bytes=64)
         bias_cols = keep.tile([P, N_TILES], F32, name="bias_cols")
@@ -63,11 +62,14 @@ def tile_list_peering_request_board_kernel(
         half = PASS // 2
         wb_raw = {}
 
-        def load_wb(b):
-            for u in range(2):
-                wb_raw[b, u] = keep.tile([P, PACK, half], F32, name=f"wb_raw{b}{u}", tag=f"wb_raw{b}{u}", align_bytes=64)
-                c0 = b * PASS + u * half
-                nc.sync.dma_start(out=wb_raw[b, u][:], in_=wb_rows[:, :, c0 : c0 + half])
+        def load_wb(b, pieces):
+            width = PASS // pieces
+            for i in range(pieces):
+                raw = keep.tile([P, PACK, width], F32, name=f"wb_raw{b}{i}", tag=f"wb_raw{b}{i}", align_bytes=64)
+                c0 = b * PASS + i * width
+                nc.sync.dma_start(out=raw[:], in_=wb_rows[:, :, c0 : c0 + width])
+                for u in range(2 // pieces):
+                    wb_raw[b, i + u] = raw[:, :, u * half : (u + 1) * half]
 
         def load_small():
             nc.sync.dma_start(board_list[:], offs3)
@@ -92,11 +94,11 @@ def tile_list_peering_request_board_kernel(
                     wc_raw[n0 + i, b] = raw[:, :, i * P : (i + 1) * P]
 
         wgo_sb = keep.tile([P, S], F32, name="wgo_sb")
-        load_wb(0)
-        load_wb(1)
+        load_wb(0, 2)
+        load_wb(1, 1)
         load_wa()
         load_tab()
-        load_wb(2)
+        load_wb(2, 2)
         load_wc(0, 1)
         load_small()
         nc.sync.dma_start(out=wgo_sb[:, 0:CHUNK], in_=wgo[:, 0:CHUNK])
@@ -124,12 +126,15 @@ def tile_list_peering_request_board_kernel(
 
         wb_codes, wb_plane = {}, {}
 
-        def quantise_wb(b):
+        def quantise_wb(b, on_vector=()):
             grouped = keep.tile([P, PACK, P, PACK], BF16, name=f"wb_grouped{b}", tag=f"wb_grouped{b}", align_bytes=64)
             for u in range(2):
-                dst = grouped[:, :, u * (P // 2) : (u + 1) * (P // 2), :].rearrange("p t m j -> p m t j")
-                src = wb_raw[b, u][:].rearrange("p j (m t) -> p m t j", t=PACK)
-                nc.scalar.activation(out=dst, in_=src, func=ACT.Copy, scale=-1.0)
+                dst = grouped[:, :, u * (P // 2) : (u + 1) * (P // 2), :].rearrange("p t m j -> p m j t")
+                src = wb_raw[b, u].rearrange("p j (m t) -> p m j t", t=PACK)
+                if u in on_vector:
+                    nc.vector.tensor_scalar(out=dst, in0=src, scalar1=-1.0, scalar2=None, op0=ALU.mult)
+                else:
+                    nc.scalar.activation(out=dst, in_=src, func=ACT.Copy, scale=-1.0)
             wb_codes[b] = keep.tile([P, PASS], U32, name=f"wb_codes{b}", align_bytes=64)
             wb_plane[b] = keep.tile([P, PASS], U8, name=f"wb_plane{b}", align_bytes=64)
             nc.vector.quantize_mx(
@@ -138,19 +143,24 @@ def tile_list_peering_request_board_kernel(
 
         wc_codes, wc_plane = {}, {}
 
-        def quantise_wc(n):
-            grouped = ring.tile([P, R_PASSES, P, PACK], BF16, name="wc_grouped", align_bytes=64)
+        def quantise_wc(n, on_vector=(), slot=None, beside=None):
+            grouped = keep.tile([P, R_PASSES, P, PACK], BF16, name=f"wc_grouped{n}", tag=slot or f"wc_grouped{n}", align_bytes=64)
             for b in range(R_PASSES):
-                nc.scalar.activation(
-                    out=grouped[:, b, :, :].rearrange("p (c i) j -> p c j i", i=4),
-                    in_=wc_raw[n, b].rearrange("p j (c i) -> p c j i", i=4),
-                    func=ACT.Copy,
-                )
+                dst = grouped[:, b, :, :].rearrange("p (c i) j -> p c j i", i=4)
+                src = wc_raw[n, b].rearrange("p j (c i) -> p c j i", i=4)
+                if b in on_vector:
+                    nc.vector.tensor_copy(out=dst, in_=src)
+                else:
+                    nc.scalar.activation(out=dst, in_=src, func=ACT.Copy)
+                if beside is not None and b < R_PASSES - 1:
+                    gap_pass(beside, b)
             wc_codes[n] = keep.tile([P, R_PASSES * P], U32, name=f"wc_codes{n}", align_bytes=64)
             wc_plane[n] = keep.tile([P, R_PASSES * P], U8, name=f"wc_plane{n}", align_bytes=64)
             nc.vector.quantize_mx(
                 out=wc_codes[n][:].bitcast(E4M3), scales=wc_plane[n][:], in_=grouped[:].rearrange("p b n j -> p (b n j)")
             )
+            if beside is not None:
+                gap_pass(beside, R_PASSES - 1)
 
         looked_up = {}
 
@@ -161,9 +171,11 @@ def tile_list_peering_request_board_kernel(
             for i in range(count):
                 looked_up[kind, c0 + i] = picked[:, i * CHUNK : (i + 1) * CHUNK]
 
-        def gather_scales(c0, count, slots):
-            gather("req_plane", tab_plane[:], req_list, U8, c0, count, slots[0])
-            gather("peer_plane", tab_plane[:], peer_list, U8, c0, count, slots[1])
+        def gather_req_scales(c0, count, slot):
+            gather("req_plane", tab_plane[:], req_list, U8, c0, count, slot)
+
+        def gather_peer_scales(c0, count, slot):
+            gather("peer_plane", tab_plane[:], peer_list, U8, c0, count, slot)
 
         def gather_req(c0, count, slot):
             gather("req_codes", tab_codes[:].bitcast(U32), req_list, U32, c0, count, slot)
@@ -229,7 +241,7 @@ def tile_list_peering_request_board_kernel(
                         stop=(b == R_PASSES - 1),
                     )
             width = count * CHUNK
-            y = keep.tile([P, width], F32, name=f"y{n}{c0}")
+            y = keep.tile([P, width], F32, name=f"y{n}{c0}", tag=f"y{n}{c0}", align_bytes=64)
             nc.scalar.activation(out=y[:], in_=bank[:, 0:width], func=ACT.Tanh, bias=bias_cols[:, n : n + 1])
             first = c0 * CHUNK
             places = board_list[:, first // 16 : (first + width) // 16]
@@ -237,30 +249,32 @@ def tile_list_peering_request_board_kernel(
             if c0 + count == CHUNKS:
                 nc.sync.dma_start(out=out[n * P : (n + 1) * P, :], in_=pages[n % len(pages)][:])
 
-        gather_scales(0, 2, ("rp0", "pp0"))
+        gather_req_scales(0, 2, "rp0")
+        gather_peer_scales(0, 2, "pp0")
         quantise_wb(0)
-        deal_wa(0)
-        quantise_wb(1)
-        deal_wa(1)
-        deal_wa(2)
         gather_req(0, 1, "rc0")
         gather_peer(0, 1, "pc0")
-        quantise_wb(2)
-        gather_req(1, 1, "rc1")
-        gather_peer(1, 1, "pc1")
+        deal_wa(0)
+        deal_wa(1)
+        deal_wa(2)
+        quantise_wb(1)
+        quantise_wb(2, ())
         gap_pass(0, 0)
         gap_pass(0, 1)
-        quantise_wc(0)
+        quantise_wc(0, (0, 1, 2))
         gap_pass(0, 2)
-        gather_scales(2, 2, ("wb_grouped2", "wb_raw21"))
-        quantise_wc(1)
+        gather_req(1, 1, "rc1")
+        gather_peer(1, 1, "pc1")
         place(0, 0, 1)
-        gather_req(2, 2, "h_grouped02")
+        quantise_wc(1)
         place(1, 0, 1)
         gap_chunk(1)
-        gather_peer(2, 2, "h_grouped12")
         place(0, 1, 1)
         quantise_wc(2)
+        gather_req_scales(2, 2, "wb_grouped2")
+        gather_peer_scales(2, 2, "wc_grouped0")
+        gather_req(2, 2, "h_grouped02")
+        gather_peer(2, 2, "h_grouped12")
         place(1, 1, 1)
         place(2, 0, 1)
         gap_chunk(2)

@@ -116,12 +116,12 @@ def tile_list_peering_request_board_kernel(
             wa_plane[b] = keep.tile([P, PASS], U8, name=f"wa_plane{b}", align_bytes=64)
             cols = slice(b * PASS, (b + 1) * PASS)
             nc.vector.tensor_copy(
-                out=wa_codes[b][:].bitcast(U16).rearrange("p (t m) -> p m t", t=PACK),
-                in_=wa_raw[:].bitcast(U16)[:, cols].rearrange("p (m t) -> p m t", t=PACK),
+                out=wa_codes[b][:].bitcast(U16).rearrange("p (t g i) -> p g t i", t=PACK, i=8),
+                in_=wa_raw[:].bitcast(U16)[:, cols].rearrange("p (g i t) -> p g t i", t=PACK, i=8),
             )
             nc.vector.tensor_copy(
-                out=wa_plane[b][:].rearrange("p (t m) -> p m t", t=PACK),
-                in_=wa_plane_raw[:, cols].rearrange("p (m t) -> p m t", t=PACK),
+                out=wa_plane[b][:].rearrange("p (t g i) -> p g t i", t=PACK, i=16),
+                in_=wa_plane_raw[:, cols].rearrange("p (g i t) -> p g t i", t=PACK, i=16),
             )
 
         wb_codes, wb_plane = {}, {}

@@ -21,11 +21,14 @@ PACK = 4
 PASS = P * PACK
 R_PASSES = H // PASS
 N_TILES = N // P
+ENTRIES_PER_COLUMN = 16
+LINE = 16
 CHUNK = 256
 CHUNKS = S // CHUNK
 SUB = 128
 GAP_BANKS = 6
 FEATURE_BANKS = 2
+PAGES = N_TILES - 1
 
 
 def tile_list_peering_request_board_kernel(
@@ -36,21 +39,21 @@ def tile_list_peering_request_board_kernel(
         keep = ctx.enter_context(tc.tile_pool(name="keep", bufs=1))
         psum = ctx.enter_context(tc.psum_pool(name="psum", bufs=1))
 
-        req_list = keep.tile([P, S // 16], U16, name="req_list")
-        peer_list = keep.tile([P, S // 16], U16, name="peer_list")
-        board_list = keep.tile([P, S // 16], U16, name="board_list")
+        req_list = keep.tile([P, S // ENTRIES_PER_COLUMN], U16, name="req_list")
+        peer_list = keep.tile([P, S // ENTRIES_PER_COLUMN], U16, name="peer_list")
+        board_list = keep.tile([P, S // ENTRIES_PER_COLUMN], U16, name="board_list")
         tab_plane = keep.tile([P, T], U8, name="tab_plane", align_bytes=64)
-        wa_plane_raw = keep.tile([P, H], U8, name="wa_plane_raw", tag="wa_plane_raw", align_bytes=64)
+        wa_plane_raw = keep.tile([P, H], U8, name="wa_plane_raw", align_bytes=64)
         tab_codes = keep.tile([P, T], I32, name="tab_codes", align_bytes=64)
         wa_raw = keep.tile([P, 2 * H], U8, name="wa_raw", align_bytes=64)
         bias_cols = keep.tile([P, N_TILES], F32, name="bias_cols")
-        pages = [keep.tile([P, T2], F32, name=f"page{n}") for n in range(N_TILES - 1)]
+        pages = [keep.tile([P, T2], F32, name=f"page{n}") for n in range(PAGES)]
         gap_banks = [psum.tile([P, PACK, SUB], F32, name=f"gap_bank{i}") for i in range(GAP_BANKS)]
         feature_banks = [psum.tile([P, 2 * CHUNK], F32, name=f"feature_bank{i}") for i in range(FEATURE_BANKS)]
 
         def load_scale_rows(queue, plane, rows):
-            for q in range(4):
-                queue.dma_start(out=plane[32 * q : 32 * q + 4, :].bitcast(I32), in_=rows[0, 4 * q : 4 * q + 4, :].bitcast(I32))
+            for i in range(4):
+                queue.dma_start(out=plane[i:P:32, :].bitcast(I32), in_=rows[0, i:16:4, :].bitcast(I32))
 
         nc.gpsimd.memset(tab_plane[:].bitcast(I32), 0)
         nc.gpsimd.memset(wa_plane_raw[:].bitcast(I32), 0)
@@ -65,23 +68,11 @@ def tile_list_peering_request_board_kernel(
         def load_wb(b, pieces):
             width = PASS // pieces
             for i in range(pieces):
-                raw = keep.tile([P, PACK, width], F32, name=f"wb_raw{b}{i}", tag=f"wb_raw{b}{i}", align_bytes=64)
+                raw = keep.tile([P, PACK, width], F32, name=f"wb_raw{b}{i}", align_bytes=64)
                 c0 = b * PASS + i * width
                 nc.sync.dma_start(out=raw[:], in_=wb_rows[:, :, c0 : c0 + width])
                 for u in range(2 // pieces):
                     wb_raw[b, i + u] = raw[:, :, u * half : (u + 1) * half]
-
-        def load_small():
-            nc.sync.dma_start(board_list[:], offs3)
-            with nc.allow_non_contiguous_dma(reason="one bias value a partition"):
-                nc.sync.dma_start(out=bias_cols[:], in_=bias.rearrange("(n p) -> p n", p=P))
-
-        def load_wa():
-            nc.sync.dma_start(out=wa_raw[:].bitcast(I32), in_=wa_words[0].bitcast(I32))
-            load_scale_rows(nc.sync, wa_plane_raw, wa_scales)
-
-        def load_tab():
-            nc.sync.dma_start(out=tab_codes[:], in_=tab_words[0].rearrange("p t i -> p (t i)").bitcast(I32))
 
         wc_raw = {}
 
@@ -96,18 +87,21 @@ def tile_list_peering_request_board_kernel(
         wgo_sb = keep.tile([P, S], F32, name="wgo_sb")
         load_wb(0, 2)
         load_wb(1, 1)
-        load_wa()
-        load_tab()
+        nc.sync.dma_start(out=wa_raw[:].bitcast(I32), in_=wa_words[0].bitcast(I32))
+        load_scale_rows(nc.sync, wa_plane_raw, wa_scales)
+        nc.sync.dma_start(out=tab_codes[:], in_=tab_words[0].rearrange("p t i -> p (t i)").bitcast(I32))
         load_wb(2, 2)
         load_wc(0, 1)
-        load_small()
+        nc.sync.dma_start(board_list[:], offs3)
+        with nc.allow_non_contiguous_dma(reason="one bias value a partition"):
+            nc.sync.dma_start(out=bias_cols[:], in_=bias.rearrange("(n p) -> p n", p=P))
         nc.sync.dma_start(out=wgo_sb[:, 0:CHUNK], in_=wgo[:, 0:CHUNK])
         load_wc(1, 1)
         nc.sync.dma_start(out=wgo_sb[:, CHUNK:S], in_=wgo[:, CHUNK:S])
         load_wc(2, 2)
 
         for page in pages:
-            nc.vector.memset(page[:], 0.0)
+            nc.vector.memset(page[:].bitcast(I32), 0)
 
         wa_codes, wa_plane = {}, {}
 
@@ -116,25 +110,22 @@ def tile_list_peering_request_board_kernel(
             wa_plane[b] = keep.tile([P, PASS], U8, name=f"wa_plane{b}", align_bytes=64)
             cols = slice(b * PASS, (b + 1) * PASS)
             nc.vector.tensor_copy(
-                out=wa_codes[b][:].bitcast(U16).rearrange("p (t g i) -> p g t i", t=PACK, i=8),
-                in_=wa_raw[:].bitcast(U16)[:, cols].rearrange("p (g i t) -> p g t i", t=PACK, i=8),
+                out=wa_codes[b][:].bitcast(U16).rearrange("p (t g i) -> p g t i", t=PACK, i=LINE // 2),
+                in_=wa_raw[:].bitcast(U16)[:, cols].rearrange("p (g i t) -> p g t i", t=PACK, i=LINE // 2),
             )
             nc.vector.tensor_copy(
-                out=wa_plane[b][:].rearrange("p (t g i) -> p g t i", t=PACK, i=16),
-                in_=wa_plane_raw[:, cols].rearrange("p (g i t) -> p g t i", t=PACK, i=16),
+                out=wa_plane[b][:].rearrange("p (t g i) -> p g t i", t=PACK, i=LINE),
+                in_=wa_plane_raw[:, cols].rearrange("p (g i t) -> p g t i", t=PACK, i=LINE),
             )
 
         wb_codes, wb_plane = {}, {}
 
-        def quantise_wb(b, on_vector=()):
-            grouped = keep.tile([P, PACK, P, PACK], BF16, name=f"wb_grouped{b}", tag=f"wb_grouped{b}", align_bytes=64)
+        def quantise_wb(b):
+            grouped = keep.tile([P, PACK, P, PACK], BF16, name=f"wb_grouped{b}", align_bytes=64)
             for u in range(2):
                 dst = grouped[:, :, u * (P // 2) : (u + 1) * (P // 2), :].rearrange("p t m j -> p m j t")
                 src = wb_raw[b, u].rearrange("p j (m t) -> p m j t", t=PACK)
-                if u in on_vector:
-                    nc.vector.tensor_scalar(out=dst, in0=src, scalar1=-1.0, scalar2=None, op0=ALU.mult)
-                else:
-                    nc.scalar.activation(out=dst, in_=src, func=ACT.Copy, scale=-1.0)
+                nc.scalar.activation(out=dst, in_=src, func=ACT.Copy, scale=-1.0)
             wb_codes[b] = keep.tile([P, PASS], U32, name=f"wb_codes{b}", align_bytes=64)
             wb_plane[b] = keep.tile([P, PASS], U8, name=f"wb_plane{b}", align_bytes=64)
             nc.vector.quantize_mx(
@@ -143,53 +134,48 @@ def tile_list_peering_request_board_kernel(
 
         wc_codes, wc_plane = {}, {}
 
-        def quantise_wc(n, on_vector=(), slot=None, beside=None):
-            grouped = keep.tile([P, R_PASSES, P, PACK], BF16, name=f"wc_grouped{n}", tag=slot or f"wc_grouped{n}", align_bytes=64)
+        def quantise_wc(n):
+            grouped = keep.tile([P, R_PASSES, P, PACK], BF16, name=f"wc_grouped{n}", align_bytes=64)
             for b in range(R_PASSES):
-                dst = grouped[:, b, :, :].rearrange("p (c i) j -> p c j i", i=4)
-                src = wc_raw[n, b].rearrange("p j (c i) -> p c j i", i=4)
-                if b in on_vector:
+                dst = grouped[:, b, :, :].rearrange("p (c i) j -> p c j i", i=LINE // 4)
+                src = wc_raw[n, b].rearrange("p j (c i) -> p c j i", i=LINE // 4)
+                if n == 0:
                     nc.vector.tensor_copy(out=dst, in_=src)
                 else:
                     nc.scalar.activation(out=dst, in_=src, func=ACT.Copy)
-                if beside is not None and b < R_PASSES - 1:
-                    gap_pass(beside, b)
             wc_codes[n] = keep.tile([P, R_PASSES * P], U32, name=f"wc_codes{n}", align_bytes=64)
             wc_plane[n] = keep.tile([P, R_PASSES * P], U8, name=f"wc_plane{n}", align_bytes=64)
             nc.vector.quantize_mx(
                 out=wc_codes[n][:].bitcast(E4M3), scales=wc_plane[n][:], in_=grouped[:].rearrange("p b n j -> p (b n j)")
             )
-            if beside is not None:
-                gap_pass(beside, R_PASSES - 1)
 
+        sources = {
+            "req_plane": (tab_plane[:], req_list, U8),
+            "peer_plane": (tab_plane[:], peer_list, U8),
+            "req_codes": (tab_codes[:].bitcast(U32), req_list, U32),
+            "peer_codes": (tab_codes[:].bitcast(U32), peer_list, U32),
+        }
         looked_up = {}
 
-        def gather(kind, window, places, dtype, c0, count, slot):
-            picked = keep.tile([P, count * CHUNK], dtype, name=f"{kind}{c0}", tag=slot, align_bytes=64)
-            cols = slice(c0 * CHUNK // 16, (c0 + count) * CHUNK // 16)
-            nc.vector.tensor_copy(picked[:], window.indirect(places[:, cols]))
+        def list_columns(entries, first, width):
+            return entries[:, first // ENTRIES_PER_COLUMN : (first + width) // ENTRIES_PER_COLUMN]
+
+        def gather(kind, c0, count, after=None):
+            window, entries, dtype = sources[kind]
+            name = f"{kind}{c0}"
+            picked = keep.tile([P, count * CHUNK], dtype, name=name, tag=after or name, align_bytes=64)
+            nc.vector.tensor_copy(picked[:], window.indirect(list_columns(entries, c0 * CHUNK, count * CHUNK)))
             for i in range(count):
                 looked_up[kind, c0 + i] = picked[:, i * CHUNK : (i + 1) * CHUNK]
-
-        def gather_req_scales(c0, count, slot):
-            gather("req_plane", tab_plane[:], req_list, U8, c0, count, slot)
-
-        def gather_peer_scales(c0, count, slot):
-            gather("peer_plane", tab_plane[:], peer_list, U8, c0, count, slot)
-
-        def gather_req(c0, count, slot):
-            gather("req_codes", tab_codes[:].bitcast(U32), req_list, U32, c0, count, slot)
-
-        def gather_peer(c0, count, slot):
-            gather("peer_codes", tab_codes[:].bitcast(U32), peer_list, U32, c0, count, slot)
 
         h_codes, h_plane = {}, {}
         turn = {"gap": 0, "feature": 0}
 
-        def gap_pass(c, b):
+        def gap_pass(c, b, after=None):
             req, peer = looked_up["req_codes", c], looked_up["peer_codes", c]
             req_plane, peer_plane = looked_up["req_plane", c], looked_up["peer_plane", c]
-            grouped = keep.tile([P, CHUNK, PACK], BF16, name=f"h_grouped{c}{b}", tag=f"h_grouped{c}{b}", align_bytes=64)
+            name = f"h_grouped{c}{b}"
+            grouped = keep.tile([P, CHUNK, PACK], BF16, name=name, tag=after or name, align_bytes=64)
             for s in range(CHUNK // SUB):
                 bank = gap_banks[turn["gap"] % GAP_BANKS]
                 turn["gap"] = turn["gap"] + 1
@@ -206,10 +192,11 @@ def tile_list_peering_request_board_kernel(
                         stop=False,
                     )
                 for t in range(PACK):
+                    col = t * P
                     nc.tensor.matmul_mx(
                         out=bank[:, t, :],
-                        lhsT=wb_codes[b][:, t * P : (t + 1) * P].bitcast(E4M3),
-                        lhsT_scale=wb_plane[b][:, t * P : (t + 1) * P],
+                        lhsT=wb_codes[b][:, col : col + P].bitcast(E4M3),
+                        lhsT_scale=wb_plane[b][:, col : col + P],
                         rhs=peer[:, local].bitcast(E4M3),
                         rhs_scale=peer_plane[:, local],
                         start=False,
@@ -240,41 +227,40 @@ def tile_list_peering_request_board_kernel(
                         start=(b == 0),
                         stop=(b == R_PASSES - 1),
                     )
-            width = count * CHUNK
-            y = keep.tile([P, width], F32, name=f"y{n}{c0}", tag=f"y{n}{c0}", align_bytes=64)
+            first, width = c0 * CHUNK, count * CHUNK
+            y = keep.tile([P, width], F32, name=f"y{n}{c0}", align_bytes=64)
             nc.scalar.activation(out=y[:], in_=bank[:, 0:width], func=ACT.Tanh, bias=bias_cols[:, n : n + 1])
-            first = c0 * CHUNK
-            places = board_list[:, first // 16 : (first + width) // 16]
-            nc.vector.tensor_tensor(pages[n % len(pages)][:].indirect(places), y[:], wgo_sb[:, first : first + width], ALU.mult)
+            page = pages[n % PAGES]
+            places = list_columns(board_list, first, width)
+            nc.vector.tensor_tensor(page[:].indirect(places), y[:], wgo_sb[:, first : first + width], ALU.mult)
             if c0 + count == CHUNKS:
-                nc.sync.dma_start(out=out[n * P : (n + 1) * P, :], in_=pages[n % len(pages)][:])
+                nc.sync.dma_start(out=out[n * P : (n + 1) * P, :], in_=page[:])
 
-        gather_req_scales(0, 2, "rp0")
-        gather_peer_scales(0, 2, "pp0")
+        gather("req_plane", 0, CHUNKS)
+        gather("peer_plane", 0, 2)
         quantise_wb(0)
-        gather_req(0, 1, "rc0")
-        gather_peer(0, 1, "pc0")
-        deal_wa(0)
-        deal_wa(1)
-        deal_wa(2)
+        gather("req_codes", 0, 1)
+        gather("peer_codes", 0, 1)
+        for b in range(R_PASSES):
+            deal_wa(b)
         quantise_wb(1)
-        quantise_wb(2, ())
-        gap_pass(0, 0)
-        gap_pass(0, 1)
-        quantise_wc(0, (0, 1, 2))
+        quantise_wb(2)
+        gap_pass(0, 0, after="wb_raw20")
+        gap_pass(0, 1, after="wb_raw21")
+        quantise_wc(0)
         gap_pass(0, 2)
-        gather_req(1, 1, "rc1")
-        gather_peer(1, 1, "pc1")
+        gather("req_codes", 1, 1)
+        gather("peer_codes", 1, 1)
         place(0, 0, 1)
+
         quantise_wc(1)
         place(1, 0, 1)
         gap_chunk(1)
         place(0, 1, 1)
         quantise_wc(2)
-        gather_req_scales(2, 2, "wb_grouped2")
-        gather_peer_scales(2, 2, "wc_grouped0")
-        gather_req(2, 2, "h_grouped02")
-        gather_peer(2, 2, "h_grouped12")
+        gather("peer_plane", 2, 2, after="wb_grouped2")
+        gather("req_codes", 2, 2, after="h_grouped02")
+        gather("peer_codes", 2, 2, after="h_grouped12")
         place(1, 1, 1)
         place(2, 0, 1)
         gap_chunk(2)

from contextlib import ExitStack

import concourse.mybir as mybir

K, T, S, H, N, T2 = 512, 2048, 1024, 1536, 512, 2048
FLOPS = 2 * (2 * K * H * S + H * N * S)

F32 = mybir.dt.float32
BF16 = mybir.dt.bfloat16
I32 = mybir.dt.int32
U32 = mybir.dt.uint32
U16 = mybir.dt.uint16
U8 = mybir.dt.uint8
E4M3 = mybir.dt.float8_e4m3fn_x4
E2M1 = mybir.dt.float4_e2m1fn_x4
ACT = mybir.ActivationFunctionType
ALU = mybir.AluOpType

P = 128
PACK = 4
PASS = P * PACK
R_PASSES = H // PASS
N_TILES = N // P
ENTRIES_PER_COLUMN = 16
LINE = 16
CHUNK = 256
CHUNKS = S // CHUNK
SUB = 128
GAP_BANKS = 6
FEATURE_BANKS = 2
PAGES = N_TILES - 1


def tile_list_peering_request_board_kernel(
    tc, tab_words, tab_scales, offs, offs2, offs3, wa_words, wa_scales, wb, wc, bias, wgo, out
):
    nc = tc.nc
    with ExitStack() as ctx:
        keep = ctx.enter_context(tc.tile_pool(name="keep", bufs=1))
        psum = ctx.enter_context(tc.psum_pool(name="psum", bufs=1))

        req_list = keep.tile([P, S // ENTRIES_PER_COLUMN], U16, name="req_list")
        peer_list = keep.tile([P, S // ENTRIES_PER_COLUMN], U16, name="peer_list")
        board_list = keep.tile([P, S // ENTRIES_PER_COLUMN], U16, name="board_list")
        tab_plane = keep.tile([P, T], U8, name="tab_plane", align_bytes=64)
        wa_plane_raw = keep.tile([P, H], U8, name="wa_plane_raw", align_bytes=64)
        tab_codes = keep.tile([P, T], I32, name="tab_codes", align_bytes=64)
        wa_raw = keep.tile([P, 2 * H], U8, name="wa_raw", align_bytes=64)
        bias_cols = keep.tile([P, N_TILES], F32, name="bias_cols")
        pages = [keep.tile([P, T2], F32, name=f"page{n}") for n in range(PAGES)]
        gap_banks = [psum.tile([P, PACK, SUB], F32, name=f"gap_bank{i}") for i in range(GAP_BANKS)]
        feature_banks = [psum.tile([P, 2 * CHUNK], F32, name=f"feature_bank{i}") for i in range(FEATURE_BANKS)]

        def load_scale_rows(queue, plane, rows):
            for i in range(4):
                queue.dma_start(out=plane[i:P:32, :].bitcast(I32), in_=rows[0, i:16:4, :].bitcast(I32))

        nc.gpsimd.memset(tab_plane[:].bitcast(I32), 0)
        nc.gpsimd.memset(wa_plane_raw[:].bitcast(I32), 0)
        load_scale_rows(nc.scalar, tab_plane, tab_scales)
        nc.sync.dma_start(req_list[:], offs)
        nc.sync.dma_start(peer_list[:], offs2)

        wb_rows = wb.rearrange("(p j) r -> p j r", j=PACK)
        half = PASS // 2
        wb_raw = {}

        def load_wb(b, pieces):
            width = PASS // pieces
            for i in range(pieces):
                raw = keep.tile([P, PACK, width], F32, name=f"wb_raw{b}{i}", align_bytes=64)
                c0 = b * PASS + i * width
                nc.sync.dma_start(out=raw[:], in_=wb_rows[:, :, c0 : c0 + width])
                for u in range(2 // pieces):
                    wb_raw[b, i + u] = raw[:, :, u * half : (u + 1) * half]

        wc_raw = {}

        def load_wc(n0, count):
            for b in range(R_PASSES):
                raw = keep.tile([P, PACK, count * P], F32, name=f"wc_raw{n0}{b}")
                rows = wc[b * PASS : (b + 1) * PASS, n0 * P : (n0 + count) * P]
                nc.sync.dma_start(out=raw[:], in_=rows.rearrange("(p j) n -> p j n", j=PACK))
                for i in range(count):
                    wc_raw[n0 + i, b] = raw[:, :, i * P : (i + 1) * P]

        wgo_sb = keep.tile([P, S], F32, name="wgo_sb")
        load_wb(0, 2)
        load_wb(1, 1)
        nc.sync.dma_start(out=wa_raw[:].bitcast(I32), in_=wa_words[0].bitcast(I32))
        load_scale_rows(nc.sync, wa_plane_raw, wa_scales)
        nc.sync.dma_start(out=tab_codes[:], in_=tab_words[0].rearrange("p t i -> p (t i)").bitcast(I32))
        load_wb(2, 2)
        load_wc(0, 1)
        nc.sync.dma_start(board_list[:], offs3)
        with nc.allow_non_contiguous_dma(reason="one bias value a partition"):
            nc.sync.dma_start(out=bias_cols[:], in_=bias.rearrange("(n p) -> p n", p=P))
        nc.sync.dma_start(out=wgo_sb[:, 0:CHUNK], in_=wgo[:, 0:CHUNK])
        load_wc(1, 1)
        nc.sync.dma_start(out=wgo_sb[:, CHUNK:S], in_=wgo[:, CHUNK:S])
        load_wc(2, 2)

        for page in pages:
            nc.vector.memset(page[:].bitcast(I32), 0)

        wa_codes, wa_plane = {}, {}

        def deal_wa(b):
            wa_codes[b] = keep.tile([P, 2 * PASS], U8, name=f"wa_codes{b}", align_bytes=64)
            wa_plane[b] = keep.tile([P, PASS], U8, name=f"wa_plane{b}", align_bytes=64)
            cols = slice(b * PASS, (b + 1) * PASS)
            nc.vector.tensor_copy(
                out=wa_codes[b][:].bitcast(U16).rearrange("p (t g i) -> p g t i", t=PACK, i=LINE // 2),
                in_=wa_raw[:].bitcast(U16)[:, cols].rearrange("p (g i t) -> p g t i", t=PACK, i=LINE // 2),
            )
            nc.vector.tensor_copy(
                out=wa_plane[b][:].rearrange("p (t g i) -> p g t i", t=PACK, i=LINE),
                in_=wa_plane_raw[:, cols].rearrange("p (g i t) -> p g t i", t=PACK, i=LINE),
            )

        wb_codes, wb_plane = {}, {}

        def quantise_wb(b):
            grouped = keep.tile([P, PACK, P, PACK], BF16, name=f"wb_grouped{b}", align_bytes=64)
            for u in range(2):
                dst = grouped[:, :, u * (P // 2) : (u + 1) * (P // 2), :].rearrange("p t m j -> p m j t")
                src = wb_raw[b, u].rearrange("p j (m t) -> p m j t", t=PACK)
                nc.scalar.activation(out=dst, in_=src, func=ACT.Copy, scale=-1.0)
            wb_codes[b] = keep.tile([P, PASS], U32, name=f"wb_codes{b}", align_bytes=64)
            wb_plane[b] = keep.tile([P, PASS], U8, name=f"wb_plane{b}", align_bytes=64)
            nc.vector.quantize_mx(
                out=wb_codes[b][:].bitcast(E4M3), scales=wb_plane[b][:], in_=grouped[:].rearrange("p t m j -> p (t m j)")
            )

        wc_codes, wc_plane = {}, {}

        def quantise_wc(n):
            grouped = keep.tile([P, R_PASSES, P, PACK], BF16, name=f"wc_grouped{n}", align_bytes=64)
            for b in range(R_PASSES):
                dst = grouped[:, b, :, :].rearrange("p (c i) j -> p c j i", i=LINE // 4)
                src = wc_raw[n, b].rearrange("p j (c i) -> p c j i", i=LINE // 4)
                if n == 0:
                    nc.vector.tensor_copy(out=dst, in_=src)
                else:
                    nc.scalar.activation(out=dst, in_=src, func=ACT.Copy)
            wc_codes[n] = keep.tile([P, R_PASSES * P], U32, name=f"wc_codes{n}", align_bytes=64)
            wc_plane[n] = keep.tile([P, R_PASSES * P], U8, name=f"wc_plane{n}", align_bytes=64)
            nc.vector.quantize_mx(
                out=wc_codes[n][:].bitcast(E4M3), scales=wc_plane[n][:], in_=grouped[:].rearrange("p b n j -> p (b n j)")
            )

        sources = {
            "req_plane": (tab_plane[:], req_list, U8),
            "peer_plane": (tab_plane[:], peer_list, U8),
            "req_codes": (tab_codes[:].bitcast(U32), req_list, U32),
            "peer_codes": (tab_codes[:].bitcast(U32), peer_list, U32),
        }
        looked_up = {}

        def list_columns(entries, first, width):
            return entries[:, first // ENTRIES_PER_COLUMN : (first + width) // ENTRIES_PER_COLUMN]

        def gather(kind, c0, count, after=None):
            window, entries, dtype = sources[kind]
            name = f"{kind}{c0}"
            picked = keep.tile([P, count * CHUNK], dtype, name=name, tag=after or name, align_bytes=64)
            nc.vector.tensor_copy(picked[:], window.indirect(list_columns(entries, c0 * CHUNK, count * CHUNK)))
            for i in range(count):
                looked_up[kind, c0 + i] = picked[:, i * CHUNK : (i + 1) * CHUNK]

        h_codes, h_plane = {}, {}
        turn = {"gap": 0, "feature": 0}

        def gap_pass(c, b, after=None):
            req, peer = looked_up["req_codes", c], looked_up["peer_codes", c]
            req_plane, peer_plane = looked_up["req_plane", c], looked_up["peer_plane", c]
            name = f"h_grouped{c}{b}"
            grouped = keep.tile([P, CHUNK, PACK], BF16, name=name, tag=after or name, align_bytes=64)
            for s in range(CHUNK // SUB):
                bank = gap_banks[turn["gap"] % GAP_BANKS]
                turn["gap"] = turn["gap"] + 1
                local = slice(s * SUB, (s + 1) * SUB)
                for t in range(PACK):
                    col = t * P
                    nc.tensor.matmul_mx(
                        out=bank[:, t, :],
                        lhsT=wa_codes[b][:, 2 * col : 2 * (col + P)].bitcast(E2M1),
                        lhsT_scale=wa_plane[b][:, col : col + P],
                        rhs=req[:, local].bitcast(E4M3),
                        rhs_scale=req_plane[:, local],
                        start=(t == 0),
                        stop=False,
                    )
                for t in range(PACK):
                    col = t * P
                    nc.tensor.matmul_mx(
                        out=bank[:, t, :],
                        lhsT=wb_codes[b][:, col : col + P].bitcast(E4M3),
                        lhsT_scale=wb_plane[b][:, col : col + P],
                        rhs=peer[:, local].bitcast(E4M3),
                        rhs_scale=peer_plane[:, local],
                        start=False,
                        stop=(t == PACK - 1),
                    )
                nc.scalar.activation(out=grouped[:, local, :], in_=bank[:].rearrange("p t j -> p j t"), func=ACT.Abs)
            h_codes[c, b] = keep.tile([P, CHUNK], U32, name=f"h_codes{c}{b}", align_bytes=64)
            h_plane[c, b] = keep.tile([P, CHUNK], U8, name=f"h_plane{c}{b}", align_bytes=64)
            nc.vector.quantize_mx(
                out=h_codes[c, b][:].bitcast(E4M3), scales=h_plane[c, b][:], in_=grouped[:].rearrange("p j t -> p (j t)")
            )

        def gap_chunk(c):
            for b in range(R_PASSES):
                gap_pass(c, b)

        def place(n, c0, count):
            bank = feature_banks[turn["feature"] % FEATURE_BANKS]
            turn["feature"] = turn["feature"] + 1
            for i in range(count):
                for b in range(R_PASSES):
                    nc.tensor.matmul_mx(
                        out=bank[:, i * CHUNK : (i + 1) * CHUNK],
                        lhsT=wc_codes[n][:, b * P : (b + 1) * P].bitcast(E4M3),
                        lhsT_scale=wc_plane[n][:, b * P : (b + 1) * P],
                        rhs=h_codes[c0 + i, b][:].bitcast(E4M3),
                        rhs_scale=h_plane[c0 + i, b][:],
                        start=(b == 0),
                        stop=(b == R_PASSES - 1),
                    )
            first, width = c0 * CHUNK, count * CHUNK
            y = keep.tile([P, width], F32, name=f"y{n}{c0}", align_bytes=64)
            nc.scalar.activation(out=y[:], in_=bank[:, 0:width], func=ACT.Tanh, bias=bias_cols[:, n : n + 1])
            page = pages[n % PAGES]
            places = list_columns(board_list, first, width)
            nc.vector.tensor_tensor(page[:].indirect(places), y[:], wgo_sb[:, first : first + width], ALU.mult)
            if c0 + count == CHUNKS:
                nc.sync.dma_start(out=out[n * P : (n + 1) * P, :], in_=page[:])

        gather("req_plane", 0, CHUNKS)
        gather("peer_plane", 0, 2)
        quantise_wb(0)
        gather("req_codes", 0, 1)
        gather("peer_codes", 0, 1)
        for b in range(R_PASSES):
            deal_wa(b)
        quantise_wb(1)
        quantise_wb(2)
        gap_pass(0, 0, after="wb_raw20")
        gap_pass(0, 1, after="wb_raw21")
        quantise_wc(0)
        gap_pass(0, 2)
        gather("req_codes", 1, 1)
        gather("peer_codes", 1, 1)
        place(0, 0, 1)

        quantise_wc(1)
        place(1, 0, 1)
        gap_chunk(1)
        place(0, 1, 1)
        quantise_wc(2)
        gather("peer_plane", 2, 2, after="wb_grouped2")
        gather("req_codes", 2, 2, after="h_grouped02")
        gather("peer_codes", 2, 2, after="h_grouped12")
        place(1, 1, 1)
        place(2, 0, 1)
        gap_chunk(2)
        place(2, 1, 1)
        place(0, 2, 1)
        gap_chunk(3)
        place(1, 2, 1)
        place(0, 3, 1)
        quantise_wc(3)
        place(1, 3, 1)
        place(2, 2, 2)
        place(3, 0, 2)
        place(3, 2, 2)
